import numpy as np
import ml_dtypes


def mxq(x, axis, fmt="e4m3"):
    dtype, down = {"e4m3": (ml_dtypes.float8_e4m3fn, 7), "e5m2": (ml_dtypes.float8_e5m2, 14)}[fmt]
    v = np.moveaxis(np.asarray(x, np.float32).astype(ml_dtypes.bfloat16).astype(np.float64), axis, -1)
    blocks = v.reshape(v.shape[:-1] + (-1, 32))
    amax = np.abs(blocks).max(-1, keepdims=True)
    byte = np.maximum(np.where(amax > 0, np.frexp(amax)[1] - 1 + 127, 0) - down, 1)
    scale = np.exp2(byte - 127.0)
    codes = (blocks / scale).astype(np.float32).astype(dtype).astype(np.float64)
    return np.moveaxis((codes * scale).reshape(v.shape), -1, axis)


WIDE = False


def mx_kscale(k):
    if not WIDE:
        return np.ones(k)
    levels = np.array([10, -10, 5, -5, 0])
    if k % 512:
        return np.exp2(np.random.permutation(np.resize(levels, k // 32))).repeat(32)
    a = np.empty((k // 512, 16))
    for p in range(k // 512):
        a[p, :8] = np.random.permutation(np.resize(levels, 8))
        for g in range(8):
            far = levels[np.abs(levels - a[p, g]) >= 10]
            a[p, g + 8] = far[np.random.randint(len(far))]
    return np.exp2(a.ravel()).repeat(32)


BF16 = ml_dtypes.bfloat16


def bf(x):
    return np.asarray(x, np.float32).astype(BF16)


def f64(x):
    return np.asarray(x).astype(np.float64)

def planes(Y):
    n, m = Y.shape
    b = f64(bf(Y)).reshape(n // 32, 32, m)
    amax = np.abs(b).max(1)
    byte = np.clip(np.where(amax > 0, np.frexp(amax)[1] - 1 + 127 - 7, 1), 1, 254)
    codes = (b * np.exp2(127.0 - byte)[:, None, :]).reshape(n, m).astype(np.float32).astype(ml_dtypes.float8_e4m3fn).view(np.uint8)
    words = codes.reshape(n // 512, 128, 4, m).transpose(0, 1, 3, 2)
    return np.ascontiguousarray(words), np.ascontiguousarray(byte.astype(np.uint8).reshape(n // 512, 16, m))


P, D, Q = 2048, 1024, 512

def setup_inputs():
    s = mx_kscale(D)
    t = mx_kscale(P)
    passages = np.random.randn(P, D) * s[None, :] * t[:, None]
    layer1 = np.random.randn(D, Q) / np.sqrt(D) / s[:, None]
    bias1 = 0.5 * np.random.randn(P) * t
    layer2 = 1.4 * np.random.randn(P, P) / np.sqrt(P) / t[:, None]
    bias2 = 0.5 * np.random.randn(P)
    first_stage = 0.5 * np.exp(0.5 * np.random.randn(Q, P))
    gain = np.exp(0.8 * np.random.randn(P))
    return {"passages": bf(passages), "layer1": bf(layer1), "bias1": bf(bias1),
            "layer2": bf(layer2), "bias2": bf(bias2),
            "first_stage": bf(first_stage), "gain": bf(gain)}

def reference(passages, layer1, bias1, layer2, bias2, first_stage, gain):
    X, W1, W2 = f64(passages), f64(layer1), f64(layer2)
    A = mxq(X, 1, "e4m3") @ mxq(W1, 0, "e4m3")
    H = np.maximum(A + f64(bias1)[:, None], 0.0)
    Z = mxq(H, 0, "e4m3").T @ mxq(W2, 0, "e4m3")
    R = np.maximum(Z + f64(bias2)[None, :], 0.0)
    y = (R + f64(first_stage)) * f64(gain)[None, :]
    Y = y.T
    words, scales = planes(Y)
    return y, words, scales

@@ -1,0 +1,343 @@
+from contextlib import ExitStack
+
+import concourse.mybir as mybir
+from concourse.masks import make_identity
+
+P, D, Q = 2048, 1024, 512
+FLOPS = 2 * P * D * Q + 2 * Q * P * P
+
+F32 = mybir.dt.float32
+BF16 = mybir.dt.bfloat16
+I32 = mybir.dt.int32
+U32 = mybir.dt.uint32
+U8 = mybir.dt.uint8
+FP8X4 = mybir.dt.float8_e4m3fn_x4
+ACT = mybir.ActivationFunctionType
+ALU = mybir.AluOpType
+
+PARTS = 128
+SLOTS = 4
+GROUP = PARTS * SLOTS
+GROUPS = P // GROUP
+PASSES1 = D // GROUP
+UNITS = 2 * GROUPS
+QTILES = Q // PARTS
+
+
+def tile_passage_pool_reranker_h3_kernel(tc, passages, layer1, bias1, layer2, bias2, first_stage, gain,
+                                                    out_0, out_1, out_2):
+    nc = tc.nc
+    with ExitStack() as ctx:
+        keep = ctx.enter_context(tc.tile_pool(name="keep", bufs=1))
+        work = ctx.enter_context(tc.tile_pool(name="work", bufs=1))
+        psum = ctx.enter_context(tc.psum_pool(name="psum", bufs=1))
+        ctx.enter_context(tc.manual_schedule())
+
+        def bank(k):
+            return psum.tile([PARTS, GROUP], F32, tag="bank%d" % k, name="bank%d" % k)
+
+        def grouped_tile():
+            return work.tile([PARTS, 4 * GROUP], BF16, tag="grouped", name="grouped", bufs=5, align_bytes=64)
+
+        def code_tiles(name, bufs):
+            codes = work.tile([PARTS, GROUP], U32, name=name + "_codes", bufs=bufs, align_bytes=64)
+            scales = work.tile([PARTS, GROUP], U8, name=name + "_scales", bufs=bufs, align_bytes=64)
+            return codes, scales
+
+        ident = keep.tile([PARTS, PARTS], F32, name="ident")
+        make_identity(nc, ident[:])
+
+        gain_bf = keep.tile([PARTS, GROUPS, SLOTS], BF16, name="gain_bf")
+        b1 = keep.tile([PARTS, GROUPS, SLOTS], BF16, name="b1")
+        b2 = keep.tile([PARTS, GROUPS, SLOTS], BF16, name="b2")
+        gain32 = keep.tile([PARTS, GROUPS, SLOTS], F32, name="gain32")
+        for dst, vec in ((gain_bf, gain), (b1, bias1), (b2, bias2)):
+            nc.scalar.dma_start(out=dst[:], in_=vec.rearrange("(g p t) -> p g t", p=PARTS, t=SLOTS))
+
+        x_raw, w1_raw, w2_raw, fs_raw = {}, {}, {}, {}
+
+        def load_x(u):
+            g, h = divmod(u, 2)
+            x_raw[u] = keep.tile([PARTS, 2, D], BF16, name="x_raw%d" % u)
+            rows = passages[g * GROUP:(g + 1) * GROUP, :].rearrange("(m t) d -> m t d", t=SLOTS)
+            nc.sync.dma_start(out=x_raw[u][:], in_=rows[:, 2 * h:2 * h + 2, :])
+
+        def load_w1(c):
+            w1_raw[c] = keep.tile([PARTS, SLOTS, Q], BF16, name="w1_raw%d" % c)
+            nc.sync.dma_start(out=w1_raw[c][:],
+                              in_=layer1[c * GROUP:(c + 1) * GROUP, :].rearrange("(p j) q -> p j q", j=SLOTS))
+
+        def load_w2(b, g):
+            w2_raw[b, g] = keep.tile([PARTS, SLOTS, GROUP], BF16, name="w2_raw%d_%d" % (b, g))
+            rows = layer2[g * GROUP:(g + 1) * GROUP, b * GROUP:(b + 1) * GROUP]
+            nc.sync.dma_start(out=w2_raw[b, g][:], in_=rows.rearrange("(p j) n -> p j n", j=SLOTS))
+
+        def load_fs(b):
+            fs_raw[b] = keep.tile([PARTS, QTILES, GROUP], BF16, name="fs_raw%d" % b)
+            nc.sync.dma_start(out=fs_raw[b][:],
+                              in_=first_stage[:, b * GROUP:(b + 1) * GROUP].rearrange("(i q) n -> q i n", q=PARTS))
+
+        load_x(0)
+        load_w1(0)
+        load_x(1)
+        load_w1(1)
+        w2_order = [(b, g) for b in range(GROUPS) for g in range(GROUPS)]
+        for u in range(2, UNITS):
+            load_x(u)
+            load_w2(*w2_order[u - 2])
+        load_fs(0)
+        for b, g in w2_order[UNITS - 2:]:
+            load_w2(b, g)
+            if g == GROUPS - 1:
+                load_fs(b)
+
+        nc.scalar.activation(out=gain32[:], in_=gain_bf[:], func=ACT.Copy)
+
+        def copy_on(engine, out, in_):
+            if engine == "vector":
+                nc.vector.tensor_copy(out=out, in_=in_)
+            else:
+                nc.scalar.copy(out=out, in_=in_)
+
+        def interleave(engine, rows):
+            grouped = grouped_tile()
+            copy_on(engine, grouped[:].rearrange("p (c i t) -> p c t i", i=4, t=SLOTS),
+                    rows.rearrange("p t (c i) -> p c t i", i=4))
+            return grouped
+
+        def quantize(grouped, codes, scales):
+            nc.vector.quantize_mx(out=codes.bitcast(FP8X4), scales=scales, in_=grouped)
+
+        w1_codes = keep.tile([PARTS, PASSES1, Q], U32, name="w1_codes", align_bytes=64)
+        w1_scales = keep.tile([PARTS, PASSES1, Q], U8, name="w1_scales", align_bytes=64)
+        h_codes = keep.tile([PARTS, GROUPS, Q], U32, name="h_codes", align_bytes=64)
+        h_scales = keep.tile([PARTS, GROUPS, Q], U8, name="h_scales", align_bytes=64)
+        x_banks, x_grouped, x_q, a_banks, h_rows, h_grouped = {}, {}, {}, {}, {}, {}
+
+        def x_transpose(u):
+            for c in range(PASSES1):
+                x_banks[u, c] = bank(2 * (u % 2) + c)
+                for a in range(2):
+                    words = x_raw[u][:, a, :].bitcast(F32)
+                    for half in range(2):
+                        col = (2 * a + half) * PARTS
+                        nc.tensor.transpose(x_banks[u, c][:, col:col + PARTS],
+                                            words[:, 256 * c + half:256 * (c + 1):2], ident[:])
+
+        def x_evac(u, c, engine):
+            if c == 0:
+                x_grouped[u] = grouped_tile()
+            dst = x_grouped[u][:, c * 1024:(c + 1) * 1024].bitcast(F32)
+            copy_on(engine, dst.rearrange("p (a m h) -> p a m h", a=2, h=2),
+                    x_banks[u, c][:].rearrange("p (a h m) -> p a m h", a=2, h=2))
+
+        def x_quantize(u):
+            x_q[u] = code_tiles("x", 3)
+            quantize(x_grouped[u][:], x_q[u][0][:], x_q[u][1][:])
+
+        def stage1_matmul(u):
+            codes, scales = x_q[u]
+            for c in range(PASSES1):
+                for a in range(2):
+                    if c == 0:
+                        a_banks[u, a] = bank(4 + 2 * (u % 2) + a)
+                    cols = slice((2 * c + a) * PARTS, (2 * c + a + 1) * PARTS)
+                    nc.tensor.matmul_mx(out=a_banks[u, a][:], lhsT=codes[:, cols].bitcast(FP8X4),
+                                        lhsT_scale=scales[:, cols], rhs=w1_codes[:, c, :].bitcast(FP8X4),
+                                        rhs_scale=w1_scales[:, c, :], start=(c == 0), stop=(c == PASSES1 - 1))
+
+        def h_relu(u):
+            g, h = divmod(u, 2)
+            if h == 0:
+                h_rows[g] = work.tile([PARTS, SLOTS, Q], BF16, tag="h_rows", name="h_rows", bufs=2)
+            for a in range(2):
+                t = 2 * h + a
+                nc.scalar.activation(out=h_rows[g][:, t, :], in_=a_banks[u, a][:], func=ACT.Relu,
+                                     bias=b1[:, g, t:t + 1])
+
+        def h_interleave(g):
+            h_grouped[g] = interleave("vector", h_rows[g][:])
+
+        def h_quantize(g):
+            quantize(h_grouped[g][:], h_codes[:, g, :], h_scales[:, g, :])
+
+        w2_grouped, w2_q, z_banks, fs_banks, gf, relu_z, y_t, y_banks, y_grouped = {}, {}, {}, {}, {}, {}, {}, {}, {}
+        y_scales = keep.tile([PARTS, Q], U8, name="y_scales", align_bytes=64)
+
+        def w2_interleave(b, g, engine):
+            w2_grouped[b, g] = grouped_tile()
+            copy_on(engine, w2_grouped[b, g][:].rearrange("p (t m x j) -> p m j x t", t=SLOTS, x=2, j=SLOTS),
+                    w2_raw[b, g][:].rearrange("p j (m x t) -> p m j x t", x=2, t=SLOTS))
+
+        def w2_quantize(b, g):
+            w2_q[b, g] = code_tiles("w2", 7)
+            quantize(w2_grouped[b, g][:], w2_q[b, g][0][:], w2_q[b, g][1][:])
+
+        def stage2_matmul(b, g):
+            codes, scales = w2_q[b, g]
+            for t in range(SLOTS):
+                if g == 0:
+                    z_banks[b, t] = bank(t)
+                cols = slice(t * PARTS, (t + 1) * PARTS)
+                nc.tensor.matmul_mx(out=z_banks[b, t][:], lhsT=codes[:, cols].bitcast(FP8X4),
+                                    lhsT_scale=scales[:, cols], rhs=h_codes[:, g, :].bitcast(FP8X4),
+                                    rhs_scale=h_scales[:, g, :], start=(g == 0), stop=(g == GROUPS - 1))
+
+        def fs_transpose(b):
+            for half in range(2):
+                fs_banks[b, half] = bank(4 + half)
+                for i in range(QTILES):
+                    words = fs_raw[b][:, i, :].bitcast(F32)
+                    nc.tensor.transpose(fs_banks[b, half][:, i * PARTS:(i + 1) * PARTS], words[:, half:256:2],
+                                        ident[:])
+
+        def fs_scale(b):
+            for t in range(SLOTS):
+                half, e = divmod(t, 2)
+                gf[b, t] = work.tile([PARTS, Q], F32, tag="gf", name="gf", bufs=8)
+                nc.scalar.activation(out=gf[b, t][:], in_=fs_banks[b, half][:].bitcast(BF16)[:, e:2 * Q:2],
+                                     func=ACT.Copy, scale=gain32[:, b, t:t + 1])
+
+        def z_relu(b, t):
+            relu_z[b, t] = work.tile([PARTS, Q], F32, tag="relu_z", name="relu_z", bufs=6)
+            nc.scalar.activation(out=relu_z[b, t][:], in_=z_banks[b, t][:], func=ACT.Relu, bias=b2[:, b, t:t + 1])
+
+        def y_combine(b, t):
+            if t == 0:
+                y_t[b] = work.tile([PARTS, SLOTS, Q], F32, tag="y_t", name="y_t", bufs=1)
+            nc.vector.scalar_tensor_tensor(out=y_t[b][:, t, :], in0=relu_z[b, t][:], scalar=gain32[:, b, t:t + 1],
+                                           in1=gf[b, t][:], op0=ALU.mult, op1=ALU.add)
+
+        def y_transpose_one(b, i, t):
+            nc.tensor.transpose(y_banks[b, i][:, t * PARTS:(t + 1) * PARTS],
+                                y_t[b][:, t, i * PARTS:(i + 1) * PARTS], ident[:])
+
+        def y_transpose(b, i):
+            y_banks[b, i] = bank(4 + (i + 2) % 4)
+            for t in range(SLOTS):
+                y_transpose_one(b, i, t)
+
+        def y_store(b, i, engine):
+            y_out = keep.tile([PARTS, GROUP], F32, name="x_raw%d" % ((QTILES * b + i) % UNITS))
+            copy_on(engine, y_out[:].rearrange("q (p t) -> q p t", t=SLOTS),
+                    y_banks[b, i][:].rearrange("q (t p) -> q p t", t=SLOTS))
+            nc.sync.dma_start(out=out_0[i * PARTS:(i + 1) * PARTS, b * GROUP:(b + 1) * GROUP], in_=y_out[:])
+
+        def y_interleave(b):
+            y_grouped[b] = interleave("vector", y_t[b][:])
+
+        def y_quantize(b):
+            y_codes = work.tile([PARTS, Q], U32, tag="y_codes", name="y_codes", bufs=2, align_bytes=64)
+            quantize(y_grouped[b][:], y_codes[:], y_scales[SLOTS * b:PARTS, :])
+            nc.sync.dma_start(out=out_1[b].rearrange("p m t -> p (m t)").bitcast(I32), in_=y_codes[:].bitcast(I32))
+
+        x_transpose(0)
+        x_evac(0, 0, "scalar")
+        x_evac(0, 1, "scalar")
+        x_transpose(1)
+        x_evac(1, 0, "scalar")
+        x_evac(1, 1, "scalar")
+        w1_grouped = [interleave("vector", w1_raw[0][:])]
+        quantize(w1_grouped[0][:], w1_codes[:, 0, :], w1_scales[:, 0, :])
+        x_quantize(0)
+        w1_grouped.append(interleave("vector", w1_raw[1][:]))
+        quantize(w1_grouped[1][:], w1_codes[:, 1, :], w1_scales[:, 1, :])
+        x_quantize(1)
+        stage1_matmul(0)
+        h_relu(0)
+        w2_interleave(0, 0, "vector")
+        w2_quantize(0, 0)
+        w2_interleave(0, 1, "vector")
+        for u in range(2, UNITS):
+            x_transpose(u)
+            x_evac(u, 0, "scalar")
+            x_evac(u, 1, "scalar")
+            stage1_matmul(u - 1)
+            h_relu(u - 1)
+            x_quantize(u)
+            if u % 2 == 0:
+                w2_quantize(*w2_order[u // 2])
+                h_interleave(u // 2 - 1)
+            else:
+                h_quantize(u // 2 - 1)
+                w2_interleave(*w2_order[u // 2 + 1], "vector")
+        stage1_matmul(UNITS - 1)
+        h_relu(UNITS - 1)
+        stage2_matmul(0, 0)
+        fs_transpose(0)
+        stage2_matmul(0, 1)
+        w2_interleave(1, 1, "scalar")
+        fs_scale(0)
+        h_interleave(GROUPS - 1)
+        w2_quantize(1, 0)
+        h_quantize(GROUPS - 1)
+        stage2_matmul(0, 2)
+        stage2_matmul(0, 3)
+        w2_interleave(1, 2, "vector")
+        w2_quantize(1, 1)
+
+        for t in range(SLOTS):
+            z_relu(0, t)
+        fs_transpose(1)
+        w2_interleave(1, 3, "scalar")
+        fs_scale(1)
+        w2_interleave(2, 0, "vector")
+        w2_quantize(1, 2)
+        for g in range(3):
+            stage2_matmul(1, g)
+        for t in range(SLOTS):
+            y_combine(0, t)
+        y_interleave(0)
+        w2_quantize(1, 3)
+        stage2_matmul(1, 3)
+        for i in range(QTILES):
+            y_transpose(0, i)
+        for b in range(1, GROUPS - 1):
+            n = b + 1
+            for t in range(SLOTS):
+                z_relu(b, t)
+            w2_quantize(n, 0)
+            y_quantize(b - 1)
+            w2_interleave(n, 1, "vector")
+            stage2_matmul(n, 0)
+            for i in (2, 3, 0, 1):
+                y_store(b - 1, i, "scalar")
+            fs_transpose(n)
+            w2_interleave(n, 3, "scalar")
+            fs_scale(n)
+            y_combine(b, 0)
+            w2_quantize(n, 1)
+            stage2_matmul(n, 1)
+            w2_interleave(n, 2, "vector")
+            y_combine(b, 1)
+            w2_quantize(n, 2)
+            stage2_matmul(n, 2)
+            y_combine(b, 2)
+            y_combine(b, 3)
+            w2_quantize(n, 3)
+            stage2_matmul(n, 3)
+            for i in range(QTILES):
+                y_transpose(b, i)
+            if n + 1 < GROUPS:
+                w2_interleave(n + 1, 0, "vector")
+            y_interleave(b)
+        b = GROUPS - 1
+        y_quantize(b - 1)
+        for t in range(SLOTS):
+            z_relu(b, t)
+        for i in range(QTILES):
+            y_store(b - 1, i, "scalar")
+            y_banks[b, i] = bank(i)
+        for t in range(SLOTS):
+            y_combine(b, t)
+            for i in range(QTILES):
+                y_transpose_one(b, i, t)
+        y_interleave(b)
+        y_store(b, 0, "scalar")
+        y_store(b, 1, "scalar")
+        y_quantize(b)
+        for quad in range(4):
+            nc.sync.dma_start(out=out_2[:, 4 * quad:4 * quad + 4, :].bitcast(I32),
+                              in_=y_scales[32 * quad:32 * quad + 16, :].bitcast(I32))
+        y_store(b, 2, "scalar")
+        y_store(b, 3, "vector")

@@ -22,6 +22,7 @@ GROUPS = P // GROUP
 PASSES1 = D // GROUP
 UNITS = 2 * GROUPS
 QTILES = Q // PARTS
+W1_SCALAR = 128
 
 
 def tile_passage_pool_reranker_h3_kernel(tc, passages, layer1, bias1, layer2, bias2, first_stage, gain,
@@ -47,12 +48,26 @@ def tile_passage_pool_reranker_h3_kernel(tc, passages, layer1, bias1, layer2, bi
         ident = keep.tile([PARTS, PARTS], F32, name="ident")
         make_identity(nc, ident[:])
 
-        gain_bf = keep.tile([PARTS, GROUPS, SLOTS], BF16, name="gain_bf")
-        b1 = keep.tile([PARTS, GROUPS, SLOTS], BF16, name="b1")
-        b2 = keep.tile([PARTS, GROUPS, SLOTS], BF16, name="b2")
-        gain32 = keep.tile([PARTS, GROUPS, SLOTS], F32, name="gain32")
-        for dst, vec in ((gain_bf, gain), (b1, bias1), (b2, bias2)):
-            nc.scalar.dma_start(out=dst[:], in_=vec.rearrange("(g p t) -> p g t", p=PARTS, t=SLOTS))
+        zero = keep.tile([PARTS, 1], F32, name="zero")
+        nc.vector.memset(zero[:], 0.0)
+        vec_rows = keep.tile([PARTS, GROUP // 2], F32, name="vec_rows")
+        nc.scalar.activation(out=vec_rows[:], in_=zero[:].to_broadcast([PARTS, GROUP // 2]), func=ACT.Copy)
+        for k, vec in enumerate((bias1, bias2, gain)):
+            nc.scalar.dma_start(out=vec_rows[GROUPS * k:GROUPS * (k + 1), :].bitcast(BF16),
+                                in_=vec.rearrange("(g n) -> g n", n=GROUP))
+        vec_cols = keep.tile([PARTS, 3 * GROUPS, SLOTS], F32, name="vec_cols")
+        b1, b2, gain32 = (vec_cols[:, GROUPS * k:GROUPS * (k + 1), :] for k in range(3))
+
+        vec_bank = bank(7)
+
+        def transpose_vectors():
+            for half in range(2):
+                nc.tensor.transpose(vec_bank[:, half * PARTS:(half + 1) * PARTS], vec_rows[:, half:GROUP // 2:2],
+                                    ident[:])
+
+        def copy_vectors():
+            pairs = vec_bank[:, :2 * PARTS].bitcast(BF16).rearrange("p (h r e) -> p r h e", h=2, e=2)
+            nc.vector.tensor_copy(out=vec_cols[:].rearrange("p r (h e) -> p r h e", e=2), in_=pairs[:, :3 * GROUPS])
 
         x_raw, w1_raw, w2_raw, fs_raw = {}, {}, {}, {}
 
@@ -82,16 +97,17 @@ def tile_passage_pool_reranker_h3_kernel(tc, passages, layer1, bias1, layer2, bi
         load_x(1)
         load_w1(1)
         w2_order = [(b, g) for b in range(GROUPS) for g in range(GROUPS)]
-        for u in range(2, UNITS):
-            load_x(u)
-            load_w2(*w2_order[u - 2])
-        load_fs(0)
-        for b, g in w2_order[UNITS - 2:]:
-            load_w2(b, g)
-            if g == GROUPS - 1:
-                load_fs(b)
-
-        nc.scalar.activation(out=gain32[:], in_=gain_bf[:], func=ACT.Copy)
+        load_w2(0, 0)
+        for g in range(1, GROUPS):
+            load_x(2 * g)
+            load_w2(0, g)
+            load_x(2 * g + 1)
+        for b in range(1, GROUPS):
+            load_w2(b, 0)
+            load_fs(b - 1)
+            for g in range(1, GROUPS):
+                load_w2(b, g)
+        load_fs(GROUPS - 1)
 
         def copy_on(engine, out, in_):
             if engine == "vector":
@@ -99,10 +115,13 @@ def tile_passage_pool_reranker_h3_kernel(tc, passages, layer1, bias1, layer2, bi
             else:
                 nc.scalar.copy(out=out, in_=in_)
 
+        def interleave_columns(engine, grouped, rows, first, last):
+            copy_on(engine, grouped[:, SLOTS * first:SLOTS * last].rearrange("p (c i t) -> p c t i", i=4, t=SLOTS),
+                    rows[:, :, first:last].rearrange("p t (c i) -> p c t i", i=4))
+
         def interleave(engine, rows):
             grouped = grouped_tile()
-            copy_on(engine, grouped[:].rearrange("p (c i t) -> p c t i", i=4, t=SLOTS),
-                    rows.rearrange("p t (c i) -> p c t i", i=4))
+            interleave_columns(engine, grouped, rows, 0, Q)
             return grouped
 
         def quantize(grouped, codes, scales):
@@ -149,7 +168,7 @@ def tile_passage_pool_reranker_h3_kernel(tc, passages, layer1, bias1, layer2, bi
         def h_relu(u):
             g, h = divmod(u, 2)
             if h == 0:
-                h_rows[g] = work.tile([PARTS, SLOTS, Q], BF16, tag="h_rows", name="h_rows", bufs=2)
+                h_rows[g] = work.tile([PARTS, SLOTS, Q], BF16, tag="slot_rows", name="h_rows", bufs=2)
             for a in range(2):
                 t = 2 * h + a
                 nc.scalar.activation(out=h_rows[g][:, t, :], in_=a_banks[u, a][:], func=ACT.Relu,
@@ -162,12 +181,20 @@ def tile_passage_pool_reranker_h3_kernel(tc, passages, layer1, bias1, layer2, bi
             quantize(h_grouped[g][:], h_codes[:, g, :], h_scales[:, g, :])
 
         w2_grouped, w2_q, z_banks, fs_banks, gf, relu_z, y_t, y_banks, y_grouped = {}, {}, {}, {}, {}, {}, {}, {}, {}
+        y_out = {}
         y_scales = keep.tile([PARTS, Q], U8, name="y_scales", align_bytes=64)
 
         def w2_interleave(b, g, engine):
             w2_grouped[b, g] = grouped_tile()
             copy_on(engine, w2_grouped[b, g][:].rearrange("p (t m x j) -> p m j x t", t=SLOTS, x=2, j=SLOTS),
                     w2_raw[b, g][:].rearrange("p j (m x t) -> p m j x t", x=2, t=SLOTS))
+
+        def w2_interleave_half(b, g, half, engine):
+            if half == 0:
+                w2_grouped[b, g] = grouped_tile()
+            dst = w2_grouped[b, g][:].rearrange("p (t m x j) -> p m j x t", t=SLOTS, x=2, j=SLOTS)
+            src = w2_raw[b, g][:].rearrange("p j (m x t) -> p m j x t", x=2, t=SLOTS)
+            copy_on(engine, dst[:, :, :, :, 2 * half:2 * half + 2], src[:, :, :, :, 2 * half:2 * half + 2])
 
         def w2_quantize(b, g):
             w2_q[b, g] = code_tiles("w2", 7)
@@ -204,7 +231,7 @@ def tile_passage_pool_reranker_h3_kernel(tc, passages, layer1, bias1, layer2, bi
 
         def y_combine(b, t):
             if t == 0:
-                y_t[b] = work.tile([PARTS, SLOTS, Q], F32, tag="y_t", name="y_t", bufs=1)
+                y_t[b] = work.tile([PARTS, SLOTS, Q], F32, tag="slot_rows", name="y_t", bufs=2)
             nc.vector.scalar_tensor_tensor(out=y_t[b][:, t, :], in0=relu_z[b, t][:], scalar=gain32[:, b, t:t + 1],
                                            in1=gf[b, t][:], op0=ALU.mult, op1=ALU.add)
 
@@ -217,11 +244,16 @@ def tile_passage_pool_reranker_h3_kernel(tc, passages, layer1, bias1, layer2, bi
             for t in range(SLOTS):
                 y_transpose_one(b, i, t)
 
-        def y_store(b, i, engine):
-            y_out = keep.tile([PARTS, GROUP], F32, name="x_raw%d" % ((QTILES * b + i) % UNITS))
-            copy_on(engine, y_out[:].rearrange("q (p t) -> q p t", t=SLOTS),
+        def y_copy(b, i, engine):
+            if (b, i // 2) not in y_out:
+                y_out[b, i // 2] = keep.tile([PARTS, 2, GROUP], F32, name="x_raw%d" % (2 * b + i // 2))
+            copy_on(engine, y_out[b, i // 2][:, i % 2, :].rearrange("q (p t) -> q p t", t=SLOTS),
                     y_banks[b, i][:].rearrange("q (t p) -> q p t", t=SLOTS))
-            nc.sync.dma_start(out=out_0[i * PARTS:(i + 1) * PARTS, b * GROUP:(b + 1) * GROUP], in_=y_out[:])
+
+        def y_store(b, first, count):
+            rows = out_0[first * PARTS:(first + count) * PARTS, b * GROUP:(b + 1) * GROUP]
+            nc.sync.dma_start(out=rows.rearrange("(i q) n -> q i n", q=PARTS),
+                              in_=y_out[b, first // 2][:, first % 2:first % 2 + count, :])
 
         def y_interleave(b):
             y_grouped[b] = interleave("vector", y_t[b][:])
@@ -231,21 +263,23 @@ def tile_passage_pool_reranker_h3_kernel(tc, passages, layer1, bias1, layer2, bi
             quantize(y_grouped[b][:], y_codes[:], y_scales[SLOTS * b:PARTS, :])
             nc.sync.dma_start(out=out_1[b].rearrange("p m t -> p (m t)").bitcast(I32), in_=y_codes[:].bitcast(I32))
 
+        w1_grouped = [grouped_tile(), grouped_tile()]
         x_transpose(0)
-        x_evac(0, 0, "scalar")
-        x_evac(0, 1, "scalar")
         x_transpose(1)
-        x_evac(1, 0, "scalar")
-        x_evac(1, 1, "scalar")
-        w1_grouped = [interleave("vector", w1_raw[0][:])]
-        quantize(w1_grouped[0][:], w1_codes[:, 0, :], w1_scales[:, 0, :])
-        x_quantize(0)
-        w1_grouped.append(interleave("vector", w1_raw[1][:]))
-        quantize(w1_grouped[1][:], w1_codes[:, 1, :], w1_scales[:, 1, :])
-        x_quantize(1)
+        transpose_vectors()
+        for c in range(PASSES1):
+            interleave_columns("scalar", w1_grouped[c], w1_raw[c], 0, W1_SCALAR)
+            x_evac(c, 0, "scalar")
+            x_evac(c, 1, "scalar")
+            interleave_columns("vector", w1_grouped[c], w1_raw[c], W1_SCALAR, Q)
+            if c == 1:
+                copy_vectors()
+            quantize(w1_grouped[c][:], w1_codes[:, c, :], w1_scales[:, c, :])
+            x_quantize(c)
         stage1_matmul(0)
+        w2_interleave_half(0, 0, 0, "scalar")
+        w2_interleave_half(0, 0, 1, "vector")
         h_relu(0)
-        w2_interleave(0, 0, "vector")
         w2_quantize(0, 0)
         w2_interleave(0, 1, "vector")
         for u in range(2, UNITS):
@@ -279,17 +313,17 @@ def tile_passage_pool_reranker_h3_kernel(tc, passages, layer1, bias1, layer2, bi
         for t in range(SLOTS):
             z_relu(0, t)
         fs_transpose(1)
-        w2_interleave(1, 3, "scalar")
         fs_scale(1)
-        w2_interleave(2, 0, "vector")
+        w2_interleave(1, 3, "vector")
         w2_quantize(1, 2)
-        for g in range(3):
-            stage2_matmul(1, g)
-        for t in range(SLOTS):
-            y_combine(0, t)
-        y_interleave(0)
+        y_combine(0, 0)
         w2_quantize(1, 3)
-        stage2_matmul(1, 3)
+        for g in range(GROUPS):
+            stage2_matmul(1, g)
+        for t in range(1, SLOTS):
+            y_combine(0, t)
+        w2_interleave(2, 0, "vector")
+        y_interleave(0)
         for i in range(QTILES):
             y_transpose(0, i)
         for b in range(1, GROUPS - 1):
@@ -300,8 +334,10 @@ def tile_passage_pool_reranker_h3_kernel(tc, passages, layer1, bias1, layer2, bi
             y_quantize(b - 1)
             w2_interleave(n, 1, "vector")
             stage2_matmul(n, 0)
-            for i in (2, 3, 0, 1):
-                y_store(b - 1, i, "scalar")
+            for i in (2, 0):
+                y_copy(b - 1, i, "scalar")
+                y_copy(b - 1, i + 1, "scalar")
+                y_store(b - 1, i, 2)
             fs_transpose(n)
             w2_interleave(n, 3, "scalar")
             fs_scale(n)
@@ -322,22 +358,24 @@ def tile_passage_pool_reranker_h3_kernel(tc, passages, layer1, bias1, layer2, bi
                 w2_interleave(n + 1, 0, "vector")
             y_interleave(b)
         b = GROUPS - 1
-        y_quantize(b - 1)
         for t in range(SLOTS):
             z_relu(b, t)
         for i in range(QTILES):
-            y_store(b - 1, i, "scalar")
             y_banks[b, i] = bank(i)
         for t in range(SLOTS):
             y_combine(b, t)
+            if t == 0:
+                y_quantize(b - 1)
             for i in range(QTILES):
                 y_transpose_one(b, i, t)
+        for i in range(QTILES):
+            y_copy(b - 1, i, "scalar" if i + 1 < QTILES else "vector")
+            y_store(b - 1, i, 1)
         y_interleave(b)
-        y_store(b, 0, "scalar")
-        y_store(b, 1, "scalar")
+        for i, engine in ((0, "scalar"), (1, "scalar"), (2, "vector"), (3, "scalar")):
+            y_copy(b, i, engine)
+            y_store(b, i, 1)
         y_quantize(b)
         for quad in range(4):
             nc.sync.dma_start(out=out_2[:, 4 * quad:4 * quad + 4, :].bitcast(I32),
                               in_=y_scales[32 * quad:32 * quad + 16, :].bitcast(I32))
-        y_store(b, 2, "scalar")
-        y_store(b, 3, "vector")

@@ -313,15 +313,15 @@ def tile_passage_pool_reranker_h3_kernel(tc, passages, layer1, bias1, layer2, bi
         for t in range(SLOTS):
             z_relu(0, t)
         fs_transpose(1)
+        w2_interleave_half(1, 3, 0, "vector")
+        w2_interleave_half(1, 3, 1, "scalar")
         fs_scale(1)
-        w2_interleave(1, 3, "vector")
         w2_quantize(1, 2)
-        y_combine(0, 0)
+        for t in range(SLOTS):
+            y_combine(0, t)
         w2_quantize(1, 3)
         for g in range(GROUPS):
             stage2_matmul(1, g)
-        for t in range(1, SLOTS):
-            y_combine(0, t)
         w2_interleave(2, 0, "vector")
         y_interleave(0)
         for i in range(QTILES):
@@ -349,9 +349,9 @@ def tile_passage_pool_reranker_h3_kernel(tc, passages, layer1, bias1, layer2, bi
             w2_quantize(n, 2)
             stage2_matmul(n, 2)
             y_combine(b, 2)
-            y_combine(b, 3)
             w2_quantize(n, 3)
             stage2_matmul(n, 3)
+            y_combine(b, 3)
             for i in range(QTILES):
                 y_transpose(b, i)
             if n + 1 < GROUPS:
@@ -369,7 +369,7 @@ def tile_passage_pool_reranker_h3_kernel(tc, passages, layer1, bias1, layer2, bi
             for i in range(QTILES):
                 y_transpose_one(b, i, t)
         for i in range(QTILES):
-            y_copy(b - 1, i, "scalar" if i + 1 < QTILES else "vector")
+            y_copy(b - 1, i, "scalar")
             y_store(b - 1, i, 1)
         y_interleave(b)
         for i, engine in ((0, "scalar"), (1, "scalar"), (2, "vector"), (3, "scalar")):

from contextlib import ExitStack

import concourse.mybir as mybir
from concourse.masks import make_identity

P, D, Q = 2048, 1024, 512
FLOPS = 2 * P * D * Q + 2 * Q * P * P

F32 = mybir.dt.float32
BF16 = mybir.dt.bfloat16
I32 = mybir.dt.int32
U32 = mybir.dt.uint32
U8 = mybir.dt.uint8
FP8X4 = mybir.dt.float8_e4m3fn_x4
ACT = mybir.ActivationFunctionType
ALU = mybir.AluOpType

PARTS = 128
SLOTS = 4
GROUP = PARTS * SLOTS
GROUPS = P // GROUP
PASSES1 = D // GROUP
UNITS = 2 * GROUPS
QTILES = Q // PARTS
W1_SCALAR = 128


def tile_passage_pool_reranker_h3_kernel(tc, passages, layer1, bias1, layer2, bias2, first_stage, gain,
                                                    out_0, out_1, out_2):
    nc = tc.nc
    with ExitStack() as ctx:
        keep = ctx.enter_context(tc.tile_pool(name="keep", bufs=1))
        work = ctx.enter_context(tc.tile_pool(name="work", bufs=1))
        psum = ctx.enter_context(tc.psum_pool(name="psum", bufs=1))
        ctx.enter_context(tc.manual_schedule())

        def bank(k):
            return psum.tile([PARTS, GROUP], F32, tag="bank%d" % k, name="bank%d" % k)

        def grouped_tile():
            return work.tile([PARTS, 4 * GROUP], BF16, tag="grouped", name="grouped", bufs=5, align_bytes=64)

        def code_tiles(name, bufs):
            codes = work.tile([PARTS, GROUP], U32, name=name + "_codes", bufs=bufs, align_bytes=64)
            scales = work.tile([PARTS, GROUP], U8, name=name + "_scales", bufs=bufs, align_bytes=64)
            return codes, scales

        ident = keep.tile([PARTS, PARTS], F32, name="ident")
        make_identity(nc, ident[:])

        zero = keep.tile([PARTS, 1], F32, name="zero")
        nc.vector.memset(zero[:], 0.0)
        vec_rows = keep.tile([PARTS, GROUP // 2], F32, name="vec_rows")
        nc.scalar.activation(out=vec_rows[:], in_=zero[:].to_broadcast([PARTS, GROUP // 2]), func=ACT.Copy)
        for k, vec in enumerate((bias1, bias2, gain)):
            nc.scalar.dma_start(out=vec_rows[GROUPS * k:GROUPS * (k + 1), :].bitcast(BF16),
                                in_=vec.rearrange("(g n) -> g n", n=GROUP))
        vec_cols = keep.tile([PARTS, 3 * GROUPS, SLOTS], F32, name="vec_cols")
        b1, b2, gain32 = (vec_cols[:, GROUPS * k:GROUPS * (k + 1), :] for k in range(3))

        vec_bank = bank(7)

        def transpose_vectors():
            for half in range(2):
                nc.tensor.transpose(vec_bank[:, half * PARTS:(half + 1) * PARTS], vec_rows[:, half:GROUP // 2:2],
                                    ident[:])

        def copy_vectors():
            pairs = vec_bank[:, :2 * PARTS].bitcast(BF16).rearrange("p (h r e) -> p r h e", h=2, e=2)
            nc.vector.tensor_copy(out=vec_cols[:].rearrange("p r (h e) -> p r h e", e=2), in_=pairs[:, :3 * GROUPS])

        x_raw, w1_raw, w2_raw, fs_raw = {}, {}, {}, {}

        def load_x(u):
            g, h = divmod(u, 2)
            x_raw[u] = keep.tile([PARTS, 2, D], BF16, name="x_raw%d" % u)
            rows = passages[g * GROUP:(g + 1) * GROUP, :].rearrange("(m t) d -> m t d", t=SLOTS)
            nc.sync.dma_start(out=x_raw[u][:], in_=rows[:, 2 * h:2 * h + 2, :])

        def load_w1(c):
            w1_raw[c] = keep.tile([PARTS, SLOTS, Q], BF16, name="w1_raw%d" % c)
            nc.sync.dma_start(out=w1_raw[c][:],
                              in_=layer1[c * GROUP:(c + 1) * GROUP, :].rearrange("(p j) q -> p j q", j=SLOTS))

        def load_w2(b, g):
            w2_raw[b, g] = keep.tile([PARTS, SLOTS, GROUP], BF16, name="w2_raw%d_%d" % (b, g))
            rows = layer2[g * GROUP:(g + 1) * GROUP, b * GROUP:(b + 1) * GROUP]
            nc.sync.dma_start(out=w2_raw[b, g][:], in_=rows.rearrange("(p j) n -> p j n", j=SLOTS))

        def load_fs(b):
            fs_raw[b] = keep.tile([PARTS, QTILES, GROUP], BF16, name="fs_raw%d" % b)
            nc.sync.dma_start(out=fs_raw[b][:],
                              in_=first_stage[:, b * GROUP:(b + 1) * GROUP].rearrange("(i q) n -> q i n", q=PARTS))

        load_x(0)
        load_w1(0)
        load_x(1)
        load_w1(1)
        w2_order = [(b, g) for b in range(GROUPS) for g in range(GROUPS)]
        load_w2(0, 0)
        for g in range(1, GROUPS):
            load_x(2 * g)
            load_w2(0, g)
            load_x(2 * g + 1)
        for b in range(1, GROUPS):
            load_w2(b, 0)
            load_fs(b - 1)
            for g in range(1, GROUPS):
                load_w2(b, g)
        load_fs(GROUPS - 1)

        def copy_on(engine, out, in_):
            if engine == "vector":
                nc.vector.tensor_copy(out=out, in_=in_)
            else:
                nc.scalar.copy(out=out, in_=in_)

        def interleave_columns(engine, grouped, rows, first, last):
            copy_on(engine, grouped[:, SLOTS * first:SLOTS * last].rearrange("p (c i t) -> p c t i", i=4, t=SLOTS),
                    rows[:, :, first:last].rearrange("p t (c i) -> p c t i", i=4))

        def interleave(engine, rows):
            grouped = grouped_tile()
            interleave_columns(engine, grouped, rows, 0, Q)
            return grouped

        def quantize(grouped, codes, scales):
            nc.vector.quantize_mx(out=codes.bitcast(FP8X4), scales=scales, in_=grouped)

        w1_codes = keep.tile([PARTS, PASSES1, Q], U32, name="w1_codes", align_bytes=64)
        w1_scales = keep.tile([PARTS, PASSES1, Q], U8, name="w1_scales", align_bytes=64)
        h_codes = keep.tile([PARTS, GROUPS, Q], U32, name="h_codes", align_bytes=64)
        h_scales = keep.tile([PARTS, GROUPS, Q], U8, name="h_scales", align_bytes=64)
        x_banks, x_grouped, x_q, a_banks, h_rows, h_grouped = {}, {}, {}, {}, {}, {}

        def x_transpose(u):
            for c in range(PASSES1):
                x_banks[u, c] = bank(2 * (u % 2) + c)
                for a in range(2):
                    words = x_raw[u][:, a, :].bitcast(F32)
                    for half in range(2):
                        col = (2 * a + half) * PARTS
                        nc.tensor.transpose(x_banks[u, c][:, col:col + PARTS],
                                            words[:, 256 * c + half:256 * (c + 1):2], ident[:])

        def x_evac(u, c, engine):
            if c == 0:
                x_grouped[u] = grouped_tile()
            dst = x_grouped[u][:, c * 1024:(c + 1) * 1024].bitcast(F32)
            copy_on(engine, dst.rearrange("p (a m h) -> p a m h", a=2, h=2),
                    x_banks[u, c][:].rearrange("p (a h m) -> p a m h", a=2, h=2))

        def x_quantize(u):
            x_q[u] = code_tiles("x", 3)
            quantize(x_grouped[u][:], x_q[u][0][:], x_q[u][1][:])

        def stage1_matmul(u):
            codes, scales = x_q[u]
            for c in range(PASSES1):
                for a in range(2):
                    if c == 0:
                        a_banks[u, a] = bank(4 + 2 * (u % 2) + a)
                    cols = slice((2 * c + a) * PARTS, (2 * c + a + 1) * PARTS)
                    nc.tensor.matmul_mx(out=a_banks[u, a][:], lhsT=codes[:, cols].bitcast(FP8X4),
                                        lhsT_scale=scales[:, cols], rhs=w1_codes[:, c, :].bitcast(FP8X4),
                                        rhs_scale=w1_scales[:, c, :], start=(c == 0), stop=(c == PASSES1 - 1))

        def h_relu(u):
            g, h = divmod(u, 2)
            if h == 0:
                h_rows[g] = work.tile([PARTS, SLOTS, Q], BF16, tag="slot_rows", name="h_rows", bufs=2)
            for a in range(2):
                t = 2 * h + a
                nc.scalar.activation(out=h_rows[g][:, t, :], in_=a_banks[u, a][:], func=ACT.Relu,
                                     bias=b1[:, g, t:t + 1])

        def h_interleave(g):
            h_grouped[g] = interleave("vector", h_rows[g][:])

        def h_quantize(g):
            quantize(h_grouped[g][:], h_codes[:, g, :], h_scales[:, g, :])

        w2_grouped, w2_q, z_banks, fs_banks, gf, relu_z, y_t, y_banks, y_grouped = {}, {}, {}, {}, {}, {}, {}, {}, {}
        y_out = {}
        y_scales = keep.tile([PARTS, Q], U8, name="y_scales", align_bytes=64)

        def w2_interleave(b, g, engine):
            w2_grouped[b, g] = grouped_tile()
            copy_on(engine, w2_grouped[b, g][:].rearrange("p (t m x j) -> p m j x t", t=SLOTS, x=2, j=SLOTS),
                    w2_raw[b, g][:].rearrange("p j (m x t) -> p m j x t", x=2, t=SLOTS))

        def w2_interleave_half(b, g, half, engine):
            if half == 0:
                w2_grouped[b, g] = grouped_tile()
            dst = w2_grouped[b, g][:].rearrange("p (t m x j) -> p m j x t", t=SLOTS, x=2, j=SLOTS)
            src = w2_raw[b, g][:].rearrange("p j (m x t) -> p m j x t", x=2, t=SLOTS)
            copy_on(engine, dst[:, :, :, :, 2 * half:2 * half + 2], src[:, :, :, :, 2 * half:2 * half + 2])

        def w2_quantize(b, g):
            w2_q[b, g] = code_tiles("w2", 7)
            quantize(w2_grouped[b, g][:], w2_q[b, g][0][:], w2_q[b, g][1][:])

        def stage2_matmul(b, g):
            codes, scales = w2_q[b, g]
            for t in range(SLOTS):
                if g == 0:
                    z_banks[b, t] = bank(t)
                cols = slice(t * PARTS, (t + 1) * PARTS)
                nc.tensor.matmul_mx(out=z_banks[b, t][:], lhsT=codes[:, cols].bitcast(FP8X4),
                                    lhsT_scale=scales[:, cols], rhs=h_codes[:, g, :].bitcast(FP8X4),
                                    rhs_scale=h_scales[:, g, :], start=(g == 0), stop=(g == GROUPS - 1))

        def fs_transpose(b):
            for half in range(2):
                fs_banks[b, half] = bank(4 + half)
                for i in range(QTILES):
                    words = fs_raw[b][:, i, :].bitcast(F32)
                    nc.tensor.transpose(fs_banks[b, half][:, i * PARTS:(i + 1) * PARTS], words[:, half:256:2],
                                        ident[:])

        def fs_scale(b):
            for t in range(SLOTS):
                half, e = divmod(t, 2)
                gf[b, t] = work.tile([PARTS, Q], F32, tag="gf", name="gf", bufs=8)
                nc.scalar.activation(out=gf[b, t][:], in_=fs_banks[b, half][:].bitcast(BF16)[:, e:2 * Q:2],
                                     func=ACT.Copy, scale=gain32[:, b, t:t + 1])

        def z_relu(b, t):
            relu_z[b, t] = work.tile([PARTS, Q], F32, tag="relu_z", name="relu_z", bufs=6)
            nc.scalar.activation(out=relu_z[b, t][:], in_=z_banks[b, t][:], func=ACT.Relu, bias=b2[:, b, t:t + 1])

        def y_combine(b, t):
            if t == 0:
                y_t[b] = work.tile([PARTS, SLOTS, Q], F32, tag="slot_rows", name="y_t", bufs=2)
            nc.vector.scalar_tensor_tensor(out=y_t[b][:, t, :], in0=relu_z[b, t][:], scalar=gain32[:, b, t:t + 1],
                                           in1=gf[b, t][:], op0=ALU.mult, op1=ALU.add)

        def y_transpose_one(b, i, t):
            nc.tensor.transpose(y_banks[b, i][:, t * PARTS:(t + 1) * PARTS],
                                y_t[b][:, t, i * PARTS:(i + 1) * PARTS], ident[:])

        def y_transpose(b, i):
            y_banks[b, i] = bank(4 + (i + 2) % 4)
            for t in range(SLOTS):
                y_transpose_one(b, i, t)

        def y_copy(b, i, engine):
            if (b, i // 2) not in y_out:
                y_out[b, i // 2] = keep.tile([PARTS, 2, GROUP], F32, name="x_raw%d" % (2 * b + i // 2))
            copy_on(engine, y_out[b, i // 2][:, i % 2, :].rearrange("q (p t) -> q p t", t=SLOTS),
                    y_banks[b, i][:].rearrange("q (t p) -> q p t", t=SLOTS))

        def y_store(b, first, count):
            rows = out_0[first * PARTS:(first + count) * PARTS, b * GROUP:(b + 1) * GROUP]
            nc.sync.dma_start(out=rows.rearrange("(i q) n -> q i n", q=PARTS),
                              in_=y_out[b, first // 2][:, first % 2:first % 2 + count, :])

        def y_interleave(b):
            y_grouped[b] = interleave("vector", y_t[b][:])

        def y_quantize(b):
            y_codes = work.tile([PARTS, Q], U32, tag="y_codes", name="y_codes", bufs=2, align_bytes=64)
            quantize(y_grouped[b][:], y_codes[:], y_scales[SLOTS * b:PARTS, :])
            nc.sync.dma_start(out=out_1[b].rearrange("p m t -> p (m t)").bitcast(I32), in_=y_codes[:].bitcast(I32))

        w1_grouped = [grouped_tile(), grouped_tile()]
        x_transpose(0)
        x_transpose(1)
        transpose_vectors()
        for c in range(PASSES1):
            interleave_columns("scalar", w1_grouped[c], w1_raw[c], 0, W1_SCALAR)
            x_evac(c, 0, "scalar")
            x_evac(c, 1, "scalar")
            interleave_columns("vector", w1_grouped[c], w1_raw[c], W1_SCALAR, Q)
            if c == 1:
                copy_vectors()
            quantize(w1_grouped[c][:], w1_codes[:, c, :], w1_scales[:, c, :])
            x_quantize(c)
        stage1_matmul(0)
        w2_interleave_half(0, 0, 0, "scalar")
        w2_interleave_half(0, 0, 1, "vector")
        h_relu(0)
        w2_quantize(0, 0)
        w2_interleave(0, 1, "vector")
        for u in range(2, UNITS):
            x_transpose(u)
            x_evac(u, 0, "scalar")
            x_evac(u, 1, "scalar")
            stage1_matmul(u - 1)
            h_relu(u - 1)
            x_quantize(u)
            if u % 2 == 0:
                w2_quantize(*w2_order[u // 2])
                h_interleave(u // 2 - 1)
            else:
                h_quantize(u // 2 - 1)
                w2_interleave(*w2_order[u // 2 + 1], "vector")
        stage1_matmul(UNITS - 1)
        h_relu(UNITS - 1)
        stage2_matmul(0, 0)
        fs_transpose(0)
        stage2_matmul(0, 1)
        w2_interleave(1, 1, "scalar")
        fs_scale(0)
        h_interleave(GROUPS - 1)
        w2_quantize(1, 0)
        h_quantize(GROUPS - 1)
        stage2_matmul(0, 2)
        stage2_matmul(0, 3)
        w2_interleave(1, 2, "vector")
        w2_quantize(1, 1)

        for t in range(SLOTS):
            z_relu(0, t)
        fs_transpose(1)
        w2_interleave_half(1, 3, 0, "vector")
        w2_interleave_half(1, 3, 1, "scalar")
        fs_scale(1)
        w2_quantize(1, 2)
        for t in range(SLOTS):
            y_combine(0, t)
        w2_quantize(1, 3)
        for g in range(GROUPS):
            stage2_matmul(1, g)
        w2_interleave(2, 0, "vector")
        y_interleave(0)
        for i in range(QTILES):
            y_transpose(0, i)
        for b in range(1, GROUPS - 1):
            n = b + 1
            for t in range(SLOTS):
                z_relu(b, t)
            w2_quantize(n, 0)
            y_quantize(b - 1)
            w2_interleave(n, 1, "vector")
            stage2_matmul(n, 0)
            for i in (2, 0):
                y_copy(b - 1, i, "scalar")
                y_copy(b - 1, i + 1, "scalar")
                y_store(b - 1, i, 2)
            fs_transpose(n)
            w2_interleave(n, 3, "scalar")
            fs_scale(n)
            y_combine(b, 0)
            w2_quantize(n, 1)
            stage2_matmul(n, 1)
            w2_interleave(n, 2, "vector")
            y_combine(b, 1)
            w2_quantize(n, 2)
            stage2_matmul(n, 2)
            y_combine(b, 2)
            w2_quantize(n, 3)
            stage2_matmul(n, 3)
            y_combine(b, 3)
            for i in range(QTILES):
                y_transpose(b, i)
            if n + 1 < GROUPS:
                w2_interleave(n + 1, 0, "vector")
            y_interleave(b)
        b = GROUPS - 1
        for t in range(SLOTS):
            z_relu(b, t)
        for i in range(QTILES):
            y_banks[b, i] = bank(i)
        for t in range(SLOTS):
            y_combine(b, t)
            if t == 0:
                y_quantize(b - 1)
            for i in range(QTILES):
                y_transpose_one(b, i, t)
        for i in range(QTILES):
            y_copy(b - 1, i, "scalar")
            y_store(b - 1, i, 1)
        y_interleave(b)
        for i, engine in ((0, "scalar"), (1, "scalar"), (2, "vector"), (3, "scalar")):
            y_copy(b, i, engine)
            y_store(b, i, 1)
        y_quantize(b)
        for quad in range(4):
            nc.sync.dma_start(out=out_2[:, 4 * quad:4 * quad + 4, :].bitcast(I32),
                              in_=y_scales[32 * quad:32 * quad + 16, :].bitcast(I32))
